import numpy as np
import ml_dtypes


def mxq(x, axis, fmt="e4m3"):
    dtype, down = {"e4m3": (ml_dtypes.float8_e4m3fn, 7), "e5m2": (ml_dtypes.float8_e5m2, 14)}[fmt]
    v = np.moveaxis(np.asarray(x, np.float32).astype(ml_dtypes.bfloat16).astype(np.float64), axis, -1)
    blocks = v.reshape(v.shape[:-1] + (-1, 32))
    amax = np.abs(blocks).max(-1, keepdims=True)
    byte = np.maximum(np.where(amax > 0, np.frexp(amax)[1] - 1 + 127, 0) - down, 1)
    scale = np.exp2(byte - 127.0)
    codes = (blocks / scale).astype(np.float32).astype(dtype).astype(np.float64)
    return np.moveaxis((codes * scale).reshape(v.shape), -1, axis)


WIDE = False


def mx_kscale(k):
    if not WIDE:
        return np.ones(k)
    levels = np.array([10, -10, 5, -5, 0])
    if k % 512:
        return np.exp2(np.random.permutation(np.resize(levels, k // 32))).repeat(32)
    a = np.empty((k // 512, 16))
    for p in range(k // 512):
        a[p, :8] = np.random.permutation(np.resize(levels, 8))
        for g in range(8):
            far = levels[np.abs(levels - a[p, g]) >= 10]
            a[p, g + 8] = far[np.random.randint(len(far))]
    return np.exp2(a.ravel()).repeat(32)


def f64(x):
    return np.asarray(x).astype(np.float64)


def striped(idx):
    return np.tile(np.asarray(idx).reshape(-1, 16).T, (8, 1)).astype(np.uint16)


def unstriped(offs):
    return offs[:16].T.reshape(-1).astype(np.int64)


E2M1 = np.array([0.0, 0.5, 1.0, 1.5, 2.0, 3.0, 4.0, 6.0, -0.0, -0.5, -1.0, -1.5, -2.0, -3.0, -4.0, -6.0])


def pack_weight(w, fmt):
    k, n = w.shape
    w = f64(np.asarray(w, np.float32).astype(ml_dtypes.bfloat16)).reshape(k // 32, 32, n)
    amax = np.abs(w).max(1)
    if fmt == "e4m3":
        byte = np.frexp(amax)[1] - 1 + 127 - 7
    else:
        mant, ex = np.frexp(amax / 6.0)
        byte = np.where(mant > 0.5, ex, ex - 1) + 127
    byte = np.clip(np.where(amax > 0, byte, 1), 1, 254)
    scaled = (w * np.exp2(127.0 - byte)[:, None, :]).reshape(k, n).astype(np.float32)
    by_word = np.ascontiguousarray(scaled.reshape(k // 512, 128, 4, n).transpose(0, 1, 3, 2))
    if fmt == "e4m3":
        words = by_word.astype(ml_dtypes.float8_e4m3fn).view(np.uint8)
    else:
        c = by_word.astype(ml_dtypes.float4_e2m1fn).view(np.uint8) & 0xF
        words = (c[..., 0::2] | (c[..., 1::2] << 4)).reshape(k // 512, 128, 2 * n)
    return np.ascontiguousarray(words), np.ascontiguousarray(byte.astype(np.uint8).reshape(k // 512, 16, n))


def unpack_weight(words, scales, fmt):
    g, _, n = scales.shape
    words = np.ascontiguousarray(words).reshape(g, 128, n, -1)
    if fmt == "e4m3":
        vals = words.view(ml_dtypes.float8_e4m3fn).astype(np.float64)
    else:
        nib = np.empty((g, 128, n, 4), np.uint8)
        nib[..., 0::2] = words & 0xF
        nib[..., 1::2] = words >> 4
        vals = E2M1[nib]
    vals = vals * np.repeat(np.exp2(scales.astype(np.float64) - 127.0), 8, axis=1)[..., None]
    return vals.transpose(0, 1, 3, 2).reshape(g * 512, n)


B, N, T, D, DV, NQ = 1, 512, 2048, 1024, 0, 128


def setup_inputs():
    n = np.random.standard_normal
    idx = np.random.permutation(T)[:B * N]
    s = mx_kscale(D)[:, None]
    kp = pack_weight(n((D, T)) / s, "e2m1")
    return {
        "qT": (n((B, D, NQ)) * s * (1.00 / np.sqrt(D))).astype(np.float32),
        "k_words": np.ascontiguousarray(kp[0].reshape(1, 2, 128, T, 2).transpose(0, 2, 3, 1, 4)).reshape(1, 128, T, 4),
        "k_scales": kp[1],
        "offs": striped(idx),
    }


def reference(qT, k_words, k_scales, offs):
    idx = unstriped(offs)
    pool = unpack_weight(k_words.reshape(1, 128, T, 2, 2).transpose(0, 3, 1, 2, 4).reshape(2, 128, 2 * T), k_scales, "e2m1")
    pick = lambda x: x[:, idx].reshape(x.shape[0], B, N).transpose(1, 0, 2)
    a = mxq(f64(qT), 1, "e4m3").transpose(0, 2, 1) @ pick(pool)
    out = np.zeros((B, NQ, T))
    for b in range(B):
        out[b][:, idx[b * N:(b + 1) * N]] = a[b]
    return out

@@ -1,0 +1,95 @@
+from contextlib import ExitStack
+
+import concourse.mybir as mybir
+
+F32 = mybir.dt.float32
+BF16 = mybir.dt.bfloat16
+I32 = mybir.dt.int32
+U32 = mybir.dt.uint32
+U16 = mybir.dt.uint16
+U8 = mybir.dt.uint8
+FP8X4 = mybir.dt.float8_e4m3fn_x4
+FP4X4 = mybir.dt.float4_e2m1fn_x4
+
+P = 128
+PACK = 4
+PASSES = 2
+SLOTS = 512
+POOL = 2048
+QUERIES = 128
+HALF = 256
+GROUP = 128
+FLOPS = 2 * QUERIES * SLOTS * PASSES * P * PACK
+
+
+def tile_attend_sddmm_kernel(tc, qT, k_words, k_scales, offs, out):
+    nc = tc.nc
+    with ExitStack() as ctx:
+        pool = ctx.enter_context(tc.tile_pool(name="pool", bufs=1))
+        psum = ctx.enter_context(tc.psum_pool(name="psum", bufs=1))
+
+        offsets = pool.tile([P, SLOTS // 16], U16, name="offsets")
+        nc.sync.dma_start(offsets[:], offs)
+
+        q_raw = pool.tile([P, PASSES, PACK, QUERIES], F32, name="q_raw")
+        q_rows = qT[0].rearrange("(o p j) n -> o p (j n)", o=PASSES, j=PACK)
+        pool_scales = pool.tile([P, POOL], U8, name="pool_scales")
+        pool_words = pool.tile([P, POOL], U32, name="pool_words")
+        nc.vector.memset(pool_scales[:].bitcast(I32), 0)
+        nc.scalar.dma_start(pool_scales[:].bitcast(I32)[0:P:4], k_scales.bitcast(I32).rearrange("o f t -> (o f) t"))
+        nc.sync.dma_start(
+            q_raw[:].rearrange("p o j n -> p o (j n)"),
+            qT[0].rearrange("(o p j) n -> p o (j n)", o=PASSES, j=PACK),
+        )
+        nc.sync.dma_start(pool_words[:].bitcast(I32), k_words[0].rearrange("p t b -> p (t b)").bitcast(I32))
+
+        planes = pool.tile([P, PASSES, SLOTS], U8, name="planes", align_bytes=64)
+        nc.vector.memset(planes[:].rearrange("p o n -> p (o n)").bitcast(I32), 0)
+        picked = pool.tile([P, SLOTS], U8, name="picked", align_bytes=64)
+        nc.vector.tensor_copy(picked[:], pool_scales[:].indirect(offsets[:]))
+        for o in range(PASSES):
+            for j in range(4):
+                queue = nc.sync if j % 2 == 0 else nc.scalar
+                first = 64 * o + 4 * j
+                queue.dma_start(planes[:, o, :].bitcast(I32)[j:P:32], picked[:].bitcast(I32)[first:first + 49:16])
+
+        row = pool.tile([P, POOL], F32, name="row")
+        nc.vector.memset(row[:], 0.0)
+
+        q_codes = pool.tile([P, PASSES, QUERIES], U32, name="q_codes", align_bytes=64)
+        q_scales = pool.tile([P, PASSES, QUERIES], U8, name="q_scales", align_bytes=64)
+        q_bf = [pool.tile([P, QUERIES, PACK], BF16, name=f"q_bf{o}", align_bytes=64) for o in range(PASSES)]
+        nc.vector.tensor_copy(q_bf[0][:], q_raw[:, 0].rearrange("p j n -> p n j"))
+        nc.scalar.copy(q_bf[1][:], q_raw[:, 1].rearrange("p j n -> p n j"))
+        for o in range(PASSES):
+            nc.vector.quantize_mx(
+                out=q_codes[:, o, :].bitcast(FP8X4),
+                scales=q_scales[:, o, :],
+                in_=q_bf[o][:].rearrange("p n j -> p (n j)"),
+            )
+
+        scores = []
+        for h in range(SLOTS // HALF):
+            cols = offsets[:, h * HALF // 16:(h + 1) * HALF // 16]
+            pairs = pool.tile([P, HALF], U32, name=f"pairs{h}", align_bytes=64)
+            nc.vector.tensor_copy(pairs[:], pool_words[:].indirect(cols))
+            words = pool.tile([P, PASSES, HALF], U16, name=f"words{h}", align_bytes=64)
+            nc.vector.tensor_copy(words[:], pairs[:].bitcast(U16).rearrange("p (n o) -> p o n", o=PASSES))
+            staged = pool.tile([P, HALF], F32, name=f"staged{h}")
+            for g in range(HALF // GROUP):
+                acc = psum.tile([P, GROUP], F32, name=f"acc{h}_{g}")
+                for o in range(PASSES):
+                    nc.tensor.matmul_mx(
+                        out=acc[:],
+                        lhsT=q_codes[:, o, :].bitcast(FP8X4),
+                        lhsT_scale=q_scales[:, o, :],
+                        rhs=words[:, o, g * GROUP:(g + 1) * GROUP].bitcast(FP4X4),
+                        rhs_scale=planes[:, o, h * HALF + g * GROUP:h * HALF + (g + 1) * GROUP],
+                        start=(o == 0),
+                        stop=(o == PASSES - 1),
+                    )
+                nc.scalar.copy(staged[:, g * GROUP:(g + 1) * GROUP], acc[:])
+            scores.append((cols, staged))
+        for cols, staged in scores:
+            nc.vector.tensor_copy(row[:].indirect(cols), staged[:])
+        nc.sync.dma_start(out[0], row[:])

@@ -35,31 +35,34 @@ def tile_attend_sddmm_kernel(tc, qT, k_words, k_scales, offs, out):
         q_rows = qT[0].rearrange("(o p j) n -> o p (j n)", o=PASSES, j=PACK)
         pool_scales = pool.tile([P, POOL], U8, name="pool_scales")
         pool_words = pool.tile([P, POOL], U32, name="pool_words")
-        nc.vector.memset(pool_scales[:].bitcast(I32), 0)
-        nc.scalar.dma_start(pool_scales[:].bitcast(I32)[0:P:4], k_scales.bitcast(I32).rearrange("o f t -> (o f) t"))
-        nc.sync.dma_start(
-            q_raw[:].rearrange("p o j n -> p o (j n)"),
-            qT[0].rearrange("(o p j) n -> p o (j n)", o=PASSES, j=PACK),
-        )
+        nc.vector.memset(pool_scales[:].bitcast(I32)[32:64], 0)
+        nc.vector.memset(pool_scales[:].bitcast(I32)[64:P], 0)
+        nc.sync.dma_start(pool_scales[:].bitcast(I32)[0:32], k_scales.bitcast(I32).rearrange("o f t -> (o f) t"))
         nc.sync.dma_start(pool_words[:].bitcast(I32), k_words[0].rearrange("p t b -> p (t b)").bitcast(I32))
+        nc.sync.dma_start(q_raw[:, 0].rearrange("p j n -> p (j n)"), q_rows[0])
+        nc.sync.dma_start(q_raw[:, 1].rearrange("p j n -> p (j n)"), q_rows[1])
 
         planes = pool.tile([P, PASSES, SLOTS], U8, name="planes", align_bytes=64)
         nc.vector.memset(planes[:].rearrange("p o n -> p (o n)").bitcast(I32), 0)
         picked = pool.tile([P, SLOTS], U8, name="picked", align_bytes=64)
         nc.vector.tensor_copy(picked[:], pool_scales[:].indirect(offsets[:]))
+        nc.vector.tensor_copy(planes[0:32, 0, :].bitcast(I32), picked[0:32, :].bitcast(I32))
         for o in range(PASSES):
-            for j in range(4):
-                queue = nc.sync if j % 2 == 0 else nc.scalar
-                first = 64 * o + 4 * j
-                queue.dma_start(planes[:, o, :].bitcast(I32)[j:P:32], picked[:].bitcast(I32)[first:first + 49:16])
+            for quad in range(4):
+                first = 16 * o + 4 * quad
+                if first > 0:
+                    nc.sync.dma_start(
+                        planes[32 * quad:32 * quad + 4, o, :].bitcast(I32), picked[first:first + 4, :].bitcast(I32)
+                    )
 
         row = pool.tile([P, POOL], F32, name="row")
-        nc.vector.memset(row[:], 0.0)
+        for c in range(0, POOL, 2048):
+            nc.vector.memset(row[:, c:c + 2048], 0.0)
 
         q_codes = pool.tile([P, PASSES, QUERIES], U32, name="q_codes", align_bytes=64)
         q_scales = pool.tile([P, PASSES, QUERIES], U8, name="q_scales", align_bytes=64)
         q_bf = [pool.tile([P, QUERIES, PACK], BF16, name=f"q_bf{o}", align_bytes=64) for o in range(PASSES)]
-        nc.vector.tensor_copy(q_bf[0][:], q_raw[:, 0].rearrange("p j n -> p n j"))
+        nc.scalar.copy(q_bf[0][:], q_raw[:, 0].rearrange("p j n -> p n j"))
         nc.scalar.copy(q_bf[1][:], q_raw[:, 1].rearrange("p j n -> p n j"))
         for o in range(PASSES):
             nc.vector.quantize_mx(

@@ -62,37 +62,42 @@ def tile_attend_sddmm_kernel(tc, qT, k_words, k_scales, offs, out):
         q_codes = pool.tile([P, PASSES, QUERIES], U32, name="q_codes", align_bytes=64)
         q_scales = pool.tile([P, PASSES, QUERIES], U8, name="q_scales", align_bytes=64)
         q_bf = [pool.tile([P, QUERIES, PACK], BF16, name=f"q_bf{o}", align_bytes=64) for o in range(PASSES)]
-        nc.scalar.copy(q_bf[0][:], q_raw[:, 0].rearrange("p j n -> p n j"))
-        nc.scalar.copy(q_bf[1][:], q_raw[:, 1].rearrange("p j n -> p n j"))
-        for o in range(PASSES):
-            nc.vector.quantize_mx(
-                out=q_codes[:, o, :].bitcast(FP8X4),
-                scales=q_scales[:, o, :],
-                in_=q_bf[o][:].rearrange("p n j -> p (n j)"),
-            )
+        nc.scalar.copy(
+            q_bf[0][:].rearrange("p (c i) j -> p c j i", i=4), q_raw[:, 0].rearrange("p j (c i) -> p c j i", i=4)
+        )
+        nc.scalar.copy(
+            q_bf[1][:].rearrange("p (c i) j -> p c j i", i=4), q_raw[:, 1].rearrange("p j (c i) -> p c j i", i=4)
+        )
 
-        scores = []
+        pairs = []
         for h in range(SLOTS // HALF):
-            cols = offsets[:, h * HALF // 16:(h + 1) * HALF // 16]
-            pairs = pool.tile([P, HALF], U32, name=f"pairs{h}", align_bytes=64)
-            nc.vector.tensor_copy(pairs[:], pool_words[:].indirect(cols))
-            words = pool.tile([P, PASSES, HALF], U16, name=f"words{h}", align_bytes=64)
-            nc.vector.tensor_copy(words[:], pairs[:].bitcast(U16).rearrange("p (n o) -> p o n", o=PASSES))
-            staged = pool.tile([P, HALF], F32, name=f"staged{h}")
-            for g in range(HALF // GROUP):
-                acc = psum.tile([P, GROUP], F32, name=f"acc{h}_{g}")
-                for o in range(PASSES):
-                    nc.tensor.matmul_mx(
-                        out=acc[:],
-                        lhsT=q_codes[:, o, :].bitcast(FP8X4),
-                        lhsT_scale=q_scales[:, o, :],
-                        rhs=words[:, o, g * GROUP:(g + 1) * GROUP].bitcast(FP4X4),
-                        rhs_scale=planes[:, o, h * HALF + g * GROUP:h * HALF + (g + 1) * GROUP],
-                        start=(o == 0),
-                        stop=(o == PASSES - 1),
+            pairs.append(pool.tile([P, HALF], U32, name=f"pairs{h}", align_bytes=64))
+            nc.vector.tensor_copy(pairs[h][:], pool_words[:].indirect(offsets[:, h * HALF // 16:(h + 1) * HALF // 16]))
+
+        words = pool.tile([P, PASSES, SLOTS], U16, name="words", align_bytes=64)
+        accs = [psum.tile([P, GROUP], F32, name=f"acc{g}") for g in range(SLOTS // GROUP)]
+        staged = pool.tile([P, SLOTS], F32, name="staged")
+        for o in range(PASSES):
+            for h in range(SLOTS // HALF):
+                nc.vector.tensor_copy(words[:, o, h * HALF:(h + 1) * HALF], pairs[h][:].bitcast(U16)[:, o::PASSES])
+                if h == 0:
+                    nc.vector.quantize_mx(
+                        out=q_codes[:, o, :].bitcast(FP8X4),
+                        scales=q_scales[:, o, :],
+                        in_=q_bf[o][:].rearrange("p n j -> p (n j)"),
                     )
-                nc.scalar.copy(staged[:, g * GROUP:(g + 1) * GROUP], acc[:])
-            scores.append((cols, staged))
-        for cols, staged in scores:
-            nc.vector.tensor_copy(row[:].indirect(cols), staged[:])
+            for g, acc in enumerate(accs):
+                cols = slice(g * GROUP, (g + 1) * GROUP)
+                nc.tensor.matmul_mx(
+                    out=acc[:],
+                    lhsT=q_codes[:, o, :].bitcast(FP8X4),
+                    lhsT_scale=q_scales[:, o, :],
+                    rhs=words[:, o, cols].bitcast(FP4X4),
+                    rhs_scale=planes[:, o, cols],
+                    start=(o == 0),
+                    stop=(o == PASSES - 1),
+                )
+                if o == PASSES - 1:
+                    nc.scalar.copy(staged[:, cols], acc[:])
+        nc.vector.tensor_copy(row[:].indirect(offsets[:]), staged[:])
         nc.sync.dma_start(out[0], row[:])

@@ -35,15 +35,15 @@ def tile_attend_sddmm_kernel(tc, qT, k_words, k_scales, offs, out):
         q_rows = qT[0].rearrange("(o p j) n -> o p (j n)", o=PASSES, j=PACK)
         pool_scales = pool.tile([P, POOL], U8, name="pool_scales")
         pool_words = pool.tile([P, POOL], U32, name="pool_words")
-        nc.vector.memset(pool_scales[:].bitcast(I32)[32:64], 0)
-        nc.vector.memset(pool_scales[:].bitcast(I32)[64:P], 0)
+        nc.gpsimd.memset(pool_scales[:].bitcast(I32)[32:64], 0)
+        nc.gpsimd.memset(pool_scales[:].bitcast(I32)[64:P], 0)
         nc.sync.dma_start(pool_scales[:].bitcast(I32)[0:32], k_scales.bitcast(I32).rearrange("o f t -> (o f) t"))
         nc.sync.dma_start(pool_words[:].bitcast(I32), k_words[0].rearrange("p t b -> p (t b)").bitcast(I32))
         nc.sync.dma_start(q_raw[:, 0].rearrange("p j n -> p (j n)"), q_rows[0])
         nc.sync.dma_start(q_raw[:, 1].rearrange("p j n -> p (j n)"), q_rows[1])
 
         planes = pool.tile([P, PASSES, SLOTS], U8, name="planes", align_bytes=64)
-        nc.vector.memset(planes[:].rearrange("p o n -> p (o n)").bitcast(I32), 0)
+        nc.gpsimd.memset(planes[:].rearrange("p o n -> p (o n)").bitcast(I32), 0)
         picked = pool.tile([P, SLOTS], U8, name="picked", align_bytes=64)
         nc.vector.tensor_copy(picked[:], pool_scales[:].indirect(offsets[:]))
         nc.vector.tensor_copy(planes[0:32, 0, :].bitcast(I32), picked[0:32, :].bitcast(I32))
@@ -57,7 +57,7 @@ def tile_attend_sddmm_kernel(tc, qT, k_words, k_scales, offs, out):
 
         row = pool.tile([P, POOL], F32, name="row")
         for c in range(0, POOL, 2048):
-            nc.vector.memset(row[:, c:c + 2048], 0.0)
+            nc.gpsimd.memset(row[:, c:c + 2048], 0.0)
 
         q_codes = pool.tile([P, PASSES, QUERIES], U32, name="q_codes", align_bytes=64)
         q_scales = pool.tile([P, PASSES, QUERIES], U8, name="q_scales", align_bytes=64)

@@ -31,73 +31,80 @@ def tile_attend_sddmm_kernel(tc, qT, k_words, k_scales, offs, out):
         offsets = pool.tile([P, SLOTS // 16], U16, name="offsets")
         nc.sync.dma_start(offsets[:], offs)
 
-        q_raw = pool.tile([P, PASSES, PACK, QUERIES], F32, name="q_raw")
         q_rows = qT[0].rearrange("(o p j) n -> o p (j n)", o=PASSES, j=PACK)
+        q_raw = [pool.tile([P, PACK * QUERIES], F32, name=f"q_raw{o}") for o in range(PASSES)]
         pool_scales = pool.tile([P, POOL], U8, name="pool_scales")
         pool_words = pool.tile([P, POOL], U32, name="pool_words")
-        nc.gpsimd.memset(pool_scales[:].bitcast(I32)[32:64], 0)
-        nc.gpsimd.memset(pool_scales[:].bitcast(I32)[64:P], 0)
+        nc.vector.memset(pool_scales[:].bitcast(I32)[32:64], 0)
+        nc.vector.memset(pool_scales[:].bitcast(I32)[64:P], 0)
         nc.sync.dma_start(pool_scales[:].bitcast(I32)[0:32], k_scales.bitcast(I32).rearrange("o f t -> (o f) t"))
         nc.sync.dma_start(pool_words[:].bitcast(I32), k_words[0].rearrange("p t b -> p (t b)").bitcast(I32))
-        nc.sync.dma_start(q_raw[:, 0].rearrange("p j n -> p (j n)"), q_rows[0])
-        nc.sync.dma_start(q_raw[:, 1].rearrange("p j n -> p (j n)"), q_rows[1])
+        for o in range(PASSES):
+            nc.sync.dma_start(q_raw[o][:], q_rows[o])
 
-        planes = pool.tile([P, PASSES, SLOTS], U8, name="planes", align_bytes=64)
-        nc.gpsimd.memset(planes[:].rearrange("p o n -> p (o n)").bitcast(I32), 0)
+        planes = [pool.tile([P, SLOTS], U8, name=f"plane{o}", align_bytes=64) for o in range(PASSES)]
+        for o in range(PASSES):
+            nc.vector.memset(planes[o][:].bitcast(I32), 0)
         picked = pool.tile([P, SLOTS], U8, name="picked", align_bytes=64)
         nc.vector.tensor_copy(picked[:], pool_scales[:].indirect(offsets[:]))
-        nc.vector.tensor_copy(planes[0:32, 0, :].bitcast(I32), picked[0:32, :].bitcast(I32))
+        nc.vector.tensor_copy(planes[0][:].bitcast(I32)[0:32], picked[:].bitcast(I32)[0:32])
         for o in range(PASSES):
             for quad in range(4):
                 first = 16 * o + 4 * quad
                 if first > 0:
                     nc.sync.dma_start(
-                        planes[32 * quad:32 * quad + 4, o, :].bitcast(I32), picked[first:first + 4, :].bitcast(I32)
+                        planes[o][:].bitcast(I32)[32 * quad:32 * quad + 4], picked[:].bitcast(I32)[first:first + 4]
                     )
 
         row = pool.tile([P, POOL], F32, name="row")
-        for c in range(0, POOL, 2048):
-            nc.gpsimd.memset(row[:, c:c + 2048], 0.0)
+        nc.vector.memset(row[:], 0.0)
 
-        q_codes = pool.tile([P, PASSES, QUERIES], U32, name="q_codes", align_bytes=64)
-        q_scales = pool.tile([P, PASSES, QUERIES], U8, name="q_scales", align_bytes=64)
-        q_bf = [pool.tile([P, QUERIES, PACK], BF16, name=f"q_bf{o}", align_bytes=64) for o in range(PASSES)]
-        nc.scalar.copy(
-            q_bf[0][:].rearrange("p (c i) j -> p c j i", i=4), q_raw[:, 0].rearrange("p j (c i) -> p c j i", i=4)
-        )
-        nc.scalar.copy(
-            q_bf[1][:].rearrange("p (c i) j -> p c j i", i=4), q_raw[:, 1].rearrange("p j (c i) -> p c j i", i=4)
-        )
+        q_codes = [pool.tile([P, QUERIES], U32, name=f"q_codes{o}", align_bytes=64) for o in range(PASSES)]
+        q_scales = [pool.tile([P, QUERIES], U8, name=f"q_scales{o}", align_bytes=64) for o in range(PASSES)]
+        q_bf = [pool.tile([P, QUERIES * PACK], BF16, name=f"q_bf{o}", tag=f"q_bf{o}", align_bytes=64) for o in range(PASSES)]
+        for o in range(PASSES):
+            nc.scalar.copy(
+                q_bf[o][:].rearrange("p (c i j) -> p c j i", i=4, j=PACK),
+                q_raw[o][:].rearrange("p (j c i) -> p c j i", j=PACK, i=4),
+            )
 
         pairs = []
         for h in range(SLOTS // HALF):
             pairs.append(pool.tile([P, HALF], U32, name=f"pairs{h}", align_bytes=64))
             nc.vector.tensor_copy(pairs[h][:], pool_words[:].indirect(offsets[:, h * HALF // 16:(h + 1) * HALF // 16]))
 
-        words = pool.tile([P, PASSES, SLOTS], U16, name="words", align_bytes=64)
-        accs = [psum.tile([P, GROUP], F32, name=f"acc{g}") for g in range(SLOTS // GROUP)]
-        staged = pool.tile([P, SLOTS], F32, name="staged")
-        for o in range(PASSES):
-            for h in range(SLOTS // HALF):
-                nc.vector.tensor_copy(words[:, o, h * HALF:(h + 1) * HALF], pairs[h][:].bitcast(U16)[:, o::PASSES])
+        first_scores = pool.tile([P, GROUP], F32, name="first_scores")
+        other_scores = pool.tile([P, SLOTS - GROUP], F32, name="other_scores")
+        staged = [first_scores[:]] + [other_scores[:, c:c + GROUP] for c in range(0, SLOTS - GROUP, GROUP)]
+        zeros = pool.tile([P, GROUP], F32, name="zeros")
+        nc.vector.memset(zeros[:], 0.0)
+        for h in range(SLOTS // HALF):
+            tag = "words0" if h == 0 else "q_bf1"
+            words = pool.tile([P, PASSES * HALF], U16, name=f"words{h}", tag=tag, align_bytes=64)
+            nc.vector.tensor_copy(
+                words[:].rearrange("p (o n) -> p o n", o=PASSES),
+                pairs[h][:].bitcast(U16).rearrange("p (n o) -> p o n", o=PASSES),
+            )
+            accs = [psum.tile([P, GROUP], F32, name=f"acc{h}_{g}") for g in range(HALF // GROUP)]
+            order = range(PASSES) if h == 0 else reversed(range(PASSES))
+            for step, o in enumerate(order):
                 if h == 0:
-                    nc.vector.quantize_mx(
-                        out=q_codes[:, o, :].bitcast(FP8X4),
-                        scales=q_scales[:, o, :],
-                        in_=q_bf[o][:].rearrange("p n j -> p (n j)"),
+                    nc.vector.quantize_mx(out=q_codes[o][:].bitcast(FP8X4), scales=q_scales[o][:], in_=q_bf[o][:])
+                for g, acc in enumerate(accs):
+                    nc.tensor.matmul_mx(
+                        out=acc[:],
+                        lhsT=q_codes[o][:].bitcast(FP8X4),
+                        lhsT_scale=q_scales[o][:],
+                        rhs=words[:, o * HALF + g * GROUP:o * HALF + (g + 1) * GROUP].bitcast(FP4X4),
+                        rhs_scale=planes[o][:, h * HALF + g * GROUP:h * HALF + (g + 1) * GROUP],
+                        start=(step == 0),
+                        stop=(step == PASSES - 1),
                     )
-            for g, acc in enumerate(accs):
-                cols = slice(g * GROUP, (g + 1) * GROUP)
-                nc.tensor.matmul_mx(
-                    out=acc[:],
-                    lhsT=q_codes[:, o, :].bitcast(FP8X4),
-                    lhsT_scale=q_scales[:, o, :],
-                    rhs=words[:, o, cols].bitcast(FP4X4),
-                    rhs_scale=planes[:, o, cols],
-                    start=(o == 0),
-                    stop=(o == PASSES - 1),
-                )
-                if o == PASSES - 1:
-                    nc.scalar.copy(staged[:, cols], acc[:])
-        nc.vector.tensor_copy(row[:].indirect(offsets[:]), staged[:])
-        nc.sync.dma_start(out[0], row[:])
+                    if step == PASSES - 1:
+                        nc.scalar.copy(staged[h * (HALF // GROUP) + g], acc[:])
+        nc.vector.tensor_tensor(
+            row[:].indirect(offsets[:, 0:GROUP // 16]), first_scores[:], zeros[:], mybir.AluOpType.add
+        )
+        nc.vector.tensor_copy(row[:].indirect(offsets[:, GROUP // 16:SLOTS // 16]), other_scores[:])
+        nc.sync.dma_start(out[0, :, 0:POOL // 2], row[:, 0:POOL // 2])
+        nc.scalar.dma_start(out[0, :, POOL // 2:POOL], row[:, POOL // 2:POOL])

@@ -29,15 +29,15 @@ def tile_attend_sddmm_kernel(tc, qT, k_words, k_scales, offs, out):
         psum = ctx.enter_context(tc.psum_pool(name="psum", bufs=1))
 
         offsets = pool.tile([P, SLOTS // 16], U16, name="offsets")
-        nc.sync.dma_start(offsets[:], offs)
 
         q_rows = qT[0].rearrange("(o p j) n -> o p (j n)", o=PASSES, j=PACK)
         q_raw = [pool.tile([P, PACK * QUERIES], F32, name=f"q_raw{o}") for o in range(PASSES)]
-        pool_scales = pool.tile([P, POOL], U8, name="pool_scales")
+        pool_scales = pool.tile([P, POOL], U8, name="pool_scales", tag="scales_then_row")
         pool_words = pool.tile([P, POOL], U32, name="pool_words")
         nc.vector.memset(pool_scales[:].bitcast(I32)[32:64], 0)
         nc.vector.memset(pool_scales[:].bitcast(I32)[64:P], 0)
         nc.sync.dma_start(pool_scales[:].bitcast(I32)[0:32], k_scales.bitcast(I32).rearrange("o f t -> (o f) t"))
+        nc.sync.dma_start(offsets[:], offs)
         nc.sync.dma_start(pool_words[:].bitcast(I32), k_words[0].rearrange("p t b -> p (t b)").bitcast(I32))
         for o in range(PASSES):
             nc.sync.dma_start(q_raw[o][:], q_rows[o])
@@ -56,8 +56,9 @@ def tile_attend_sddmm_kernel(tc, qT, k_words, k_scales, offs, out):
                         planes[o][:].bitcast(I32)[32 * quad:32 * quad + 4], picked[:].bitcast(I32)[first:first + 4]
                     )
 
-        row = pool.tile([P, POOL], F32, name="row")
-        nc.vector.memset(row[:], 0.0)
+        row = pool.tile([P, POOL], F32, name="row", tag="scales_then_row")
+        for c in range(0, POOL, POOL // 4):
+            nc.vector.memset(row[:, c:c + POOL // 4], 0.0)
 
         q_codes = [pool.tile([P, QUERIES], U32, name=f"q_codes{o}", align_bytes=64) for o in range(PASSES)]
         q_scales = [pool.tile([P, QUERIES], U8, name=f"q_scales{o}", align_bytes=64) for o in range(PASSES)]

@@ -19,6 +19,7 @@ POOL = 2048
 QUERIES = 128
 HALF = 256
 GROUP = 128
+SCALAR_SHARE = 16
 FLOPS = 2 * QUERIES * SLOTS * PASSES * P * PACK
 
 
@@ -31,8 +32,8 @@ def tile_attend_sddmm_kernel(tc, qT, k_words, k_scales, offs, out):
         offsets = pool.tile([P, SLOTS // 16], U16, name="offsets")
 
         q_rows = qT[0].rearrange("(o p j) n -> o p (j n)", o=PASSES, j=PACK)
-        q_raw = [pool.tile([P, PACK * QUERIES], F32, name=f"q_raw{o}") for o in range(PASSES)]
-        pool_scales = pool.tile([P, POOL], U8, name="pool_scales", tag="scales_then_row")
+        q_raw = [pool.tile([P, PACK * QUERIES], F32, name=f"q_raw{o}", tag=f"q_raw{o}", align_bytes=64) for o in range(PASSES)]
+        pool_scales = pool.tile([P, POOL], U8, name="pool_scales")
         pool_words = pool.tile([P, POOL], U32, name="pool_words")
         nc.vector.memset(pool_scales[:].bitcast(I32)[32:64], 0)
         nc.vector.memset(pool_scales[:].bitcast(I32)[64:P], 0)
@@ -56,53 +57,65 @@ def tile_attend_sddmm_kernel(tc, qT, k_words, k_scales, offs, out):
                         planes[o][:].bitcast(I32)[32 * quad:32 * quad + 4], picked[:].bitcast(I32)[first:first + 4]
                     )
 
-        row = pool.tile([P, POOL], F32, name="row", tag="scales_then_row")
+        row = pool.tile([P, POOL], F32, name="row")
         for c in range(0, POOL, POOL // 4):
             nc.vector.memset(row[:, c:c + POOL // 4], 0.0)
 
         q_codes = [pool.tile([P, QUERIES], U32, name=f"q_codes{o}", align_bytes=64) for o in range(PASSES)]
         q_scales = [pool.tile([P, QUERIES], U8, name=f"q_scales{o}", align_bytes=64) for o in range(PASSES)]
         q_bf = [pool.tile([P, QUERIES * PACK], BF16, name=f"q_bf{o}", tag=f"q_bf{o}", align_bytes=64) for o in range(PASSES)]
-        for o in range(PASSES):
-            nc.scalar.copy(
-                q_bf[o][:].rearrange("p (c i j) -> p c j i", i=4, j=PACK),
-                q_raw[o][:].rearrange("p (j c i) -> p c j i", j=PACK, i=4),
+
+        def cast(copy, o, first, last):
+            copy(
+                q_bf[o][:].rearrange("p (c i j) -> p c j i", i=4, j=PACK)[:, first:last],
+                q_raw[o][:].rearrange("p (j c i) -> p c j i", j=PACK, i=4)[:, first:last],
             )
 
-        pairs = []
-        for h in range(SLOTS // HALF):
-            pairs.append(pool.tile([P, HALF], U32, name=f"pairs{h}", align_bytes=64))
-            nc.vector.tensor_copy(pairs[h][:], pool_words[:].indirect(offsets[:, h * HALF // 16:(h + 1) * HALF // 16]))
-
-        first_scores = pool.tile([P, GROUP], F32, name="first_scores")
-        other_scores = pool.tile([P, SLOTS - GROUP], F32, name="other_scores")
-        staged = [first_scores[:]] + [other_scores[:, c:c + GROUP] for c in range(0, SLOTS - GROUP, GROUP)]
-        zeros = pool.tile([P, GROUP], F32, name="zeros")
-        nc.vector.memset(zeros[:], 0.0)
-        for h in range(SLOTS // HALF):
-            tag = "words0" if h == 0 else "q_bf1"
-            words = pool.tile([P, PASSES * HALF], U16, name=f"words{h}", tag=tag, align_bytes=64)
+        def part(name, tag, first, count):
+            words = pool.tile([P, PASSES * count], U16, name=name, tag=tag, align_bytes=64)
             nc.vector.tensor_copy(
                 words[:].rearrange("p (o n) -> p o n", o=PASSES),
-                pairs[h][:].bitcast(U16).rearrange("p (n o) -> p o n", o=PASSES),
+                pairs[:, first:first + count].bitcast(U16).rearrange("p (n o) -> p o n", o=PASSES),
             )
-            accs = [psum.tile([P, GROUP], F32, name=f"acc{h}_{g}") for g in range(HALF // GROUP)]
-            order = range(PASSES) if h == 0 else reversed(range(PASSES))
+            return [words[:, o * count:(o + 1) * count] for o in range(PASSES)]
+
+        def score(name, words, first, order):
+            count = words[0].shape[1]
+            staged = pool.tile([P, count], F32, name=name)
+            accs = [psum.tile([P, GROUP], F32, name=f"acc{first + c}") for c in range(0, count, GROUP)]
             for step, o in enumerate(order):
-                if h == 0:
-                    nc.vector.quantize_mx(out=q_codes[o][:].bitcast(FP8X4), scales=q_scales[o][:], in_=q_bf[o][:])
                 for g, acc in enumerate(accs):
+                    cols = slice(g * GROUP, (g + 1) * GROUP)
                     nc.tensor.matmul_mx(
                         out=acc[:],
                         lhsT=q_codes[o][:].bitcast(FP8X4),
                         lhsT_scale=q_scales[o][:],
-                        rhs=words[:, o * HALF + g * GROUP:o * HALF + (g + 1) * GROUP].bitcast(FP4X4),
-                        rhs_scale=planes[o][:, h * HALF + g * GROUP:h * HALF + (g + 1) * GROUP],
+                        rhs=words[o][:, cols].bitcast(FP4X4),
+                        rhs_scale=planes[o][:, first + g * GROUP:first + (g + 1) * GROUP],
                         start=(step == 0),
                         stop=(step == PASSES - 1),
                     )
                     if step == PASSES - 1:
-                        nc.scalar.copy(staged[h * (HALF // GROUP) + g], acc[:])
+                        nc.scalar.copy(staged[:, cols], acc[:])
+            return staged
+
+        pairs = pool.tile([P, SLOTS], U32, name="pairs", align_bytes=64)
+        for h in range(SLOTS // HALF):
+            nc.vector.tensor_copy(
+                pairs[:, h * HALF:(h + 1) * HALF],
+                pool_words[:].indirect(offsets[:, h * HALF // 16:(h + 1) * HALF // 16]),
+            )
+        cast(nc.scalar.copy, 0, 0, QUERIES // 4)
+        cast(nc.scalar.copy, 1, 0, SCALAR_SHARE)
+        cast(nc.vector.tensor_copy, 1, SCALAR_SHARE, QUERIES // 4)
+        first_words = part("first_words", "q_raw0", 0, GROUP)
+        for o in range(PASSES):
+            nc.vector.quantize_mx(out=q_codes[o][:].bitcast(FP8X4), scales=q_scales[o][:], in_=q_bf[o][:])
+        first_scores = score("first_scores", first_words, 0, (0, 1))
+        other_words = part("other_words", "q_bf1", GROUP, SLOTS - GROUP)
+        other_scores = score("other_scores", other_words, GROUP, (1, 0))
+        zeros = pool.tile([P, GROUP], F32, name="zeros")
+        nc.vector.memset(zeros[:], 0.0)
         nc.vector.tensor_tensor(
             row[:].indirect(offsets[:, 0:GROUP // 16]), first_scores[:], zeros[:], mybir.AluOpType.add
         )

@@ -58,8 +58,7 @@ def tile_attend_sddmm_kernel(tc, qT, k_words, k_scales, offs, out):
                     )
 
         row = pool.tile([P, POOL], F32, name="row")
-        for c in range(0, POOL, POOL // 4):
-            nc.vector.memset(row[:, c:c + POOL // 4], 0.0)
+        nc.vector.memset(row[:], 0.0)
 
         q_codes = [pool.tile([P, QUERIES], U32, name=f"q_codes{o}", align_bytes=64) for o in range(PASSES)]
         q_scales = [pool.tile([P, QUERIES], U8, name=f"q_scales{o}", align_bytes=64) for o in range(PASSES)]
@@ -112,7 +111,10 @@ def tile_attend_sddmm_kernel(tc, qT, k_words, k_scales, offs, out):
         for o in range(PASSES):
             nc.vector.quantize_mx(out=q_codes[o][:].bitcast(FP8X4), scales=q_scales[o][:], in_=q_bf[o][:])
         first_scores = score("first_scores", first_words, 0, (0, 1))
-        other_words = part("other_words", "q_bf1", GROUP, SLOTS - GROUP)
+        other_tile = pool.tile([P, PASSES * (SLOTS - GROUP)], U16, name="other_words", tag="q_bf1", align_bytes=64)
+        other_words = [other_tile[:, o * (SLOTS - GROUP):(o + 1) * (SLOTS - GROUP)] for o in range(PASSES)]
+        for o in (1, 0):
+            nc.vector.tensor_copy(other_words[o], pairs[:, GROUP:SLOTS].bitcast(U16)[:, o::PASSES])
         other_scores = score("other_scores", other_words, GROUP, (1, 0))
         zeros = pool.tile([P, GROUP], F32, name="zeros")
         nc.vector.memset(zeros[:], 0.0)

@@ -111,7 +111,7 @@ def tile_attend_sddmm_kernel(tc, qT, k_words, k_scales, offs, out):
         for o in range(PASSES):
             nc.vector.quantize_mx(out=q_codes[o][:].bitcast(FP8X4), scales=q_scales[o][:], in_=q_bf[o][:])
         first_scores = score("first_scores", first_words, 0, (0, 1))
-        other_tile = pool.tile([P, PASSES * (SLOTS - GROUP)], U16, name="other_words", tag="q_bf1", align_bytes=64)
+        other_tile = pool.tile([P, PASSES * (SLOTS - GROUP)], U16, name="other_words", tag="q_raw1", align_bytes=64)
         other_words = [other_tile[:, o * (SLOTS - GROUP):(o + 1) * (SLOTS - GROUP)] for o in range(PASSES)]
         for o in (1, 0):
             nc.vector.tensor_copy(other_words[o], pairs[:, GROUP:SLOTS].bitcast(U16)[:, o::PASSES])

@@ -70,6 +70,9 @@ def tile_attend_sddmm_kernel(tc, qT, k_words, k_scales, offs, out):
                 q_raw[o][:].rearrange("p (j c i) -> p c j i", j=PACK, i=4)[:, first:last],
             )
 
+        def quantise(o):
+            nc.vector.quantize_mx(out=q_codes[o][:].bitcast(FP8X4), scales=q_scales[o][:], in_=q_bf[o][:])
+
         def part(name, tag, first, count):
             words = pool.tile([P, PASSES * count], U16, name=name, tag=tag, align_bytes=64)
             nc.vector.tensor_copy(
@@ -107,9 +110,9 @@ def tile_attend_sddmm_kernel(tc, qT, k_words, k_scales, offs, out):
         cast(nc.scalar.copy, 0, 0, QUERIES // 4)
         cast(nc.scalar.copy, 1, 0, SCALAR_SHARE)
         cast(nc.vector.tensor_copy, 1, SCALAR_SHARE, QUERIES // 4)
+        quantise(0)
         first_words = part("first_words", "q_raw0", 0, GROUP)
-        for o in range(PASSES):
-            nc.vector.quantize_mx(out=q_codes[o][:].bitcast(FP8X4), scales=q_scales[o][:], in_=q_bf[o][:])
+        quantise(1)
         first_scores = score("first_scores", first_words, 0, (0, 1))
         other_tile = pool.tile([P, PASSES * (SLOTS - GROUP)], U16, name="other_words", tag="q_raw1", align_bytes=64)
         other_words = [other_tile[:, o * (SLOTS - GROUP):(o + 1) * (SLOTS - GROUP)] for o in range(PASSES)]

@@ -125,5 +125,4 @@ def tile_attend_sddmm_kernel(tc, qT, k_words, k_scales, offs, out):
             row[:].indirect(offsets[:, 0:GROUP // 16]), first_scores[:], zeros[:], mybir.AluOpType.add
         )
         nc.vector.tensor_copy(row[:].indirect(offsets[:, GROUP // 16:SLOTS // 16]), other_scores[:])
-        nc.sync.dma_start(out[0, :, 0:POOL // 2], row[:, 0:POOL // 2])
-        nc.scalar.dma_start(out[0, :, POOL // 2:POOL], row[:, POOL // 2:POOL])
+        nc.sync.dma_start(out[0], row[:])

@@ -32,9 +32,9 @@ def tile_attend_sddmm_kernel(tc, qT, k_words, k_scales, offs, out):
         offsets = pool.tile([P, SLOTS // 16], U16, name="offsets")
 
         q_rows = qT[0].rearrange("(o p j) n -> o p (j n)", o=PASSES, j=PACK)
-        q_raw = [pool.tile([P, PACK * QUERIES], F32, name=f"q_raw{o}", tag=f"q_raw{o}", align_bytes=64) for o in range(PASSES)]
-        pool_scales = pool.tile([P, POOL], U8, name="pool_scales")
-        pool_words = pool.tile([P, POOL], U32, name="pool_words")
+        q_raw = [pool.tile([P, PACK * QUERIES], F32, name=f"q_raw{o}", tag=f"q_raw{o}", align_bytes=256) for o in range(PASSES)]
+        pool_scales = pool.tile([P, POOL], U8, name="pool_scales", align_bytes=256)
+        pool_words = pool.tile([P, POOL], U32, name="pool_words", align_bytes=256)
         nc.vector.memset(pool_scales[:].bitcast(I32)[32:64], 0)
         nc.vector.memset(pool_scales[:].bitcast(I32)[64:P], 0)
         nc.sync.dma_start(pool_scales[:].bitcast(I32)[0:32], k_scales.bitcast(I32).rearrange("o f t -> (o f) t"))
@@ -43,10 +43,10 @@ def tile_attend_sddmm_kernel(tc, qT, k_words, k_scales, offs, out):
         for o in range(PASSES):
             nc.sync.dma_start(q_raw[o][:], q_rows[o])
 
-        planes = [pool.tile([P, SLOTS], U8, name=f"plane{o}", align_bytes=64) for o in range(PASSES)]
+        planes = [pool.tile([P, SLOTS], U8, name=f"plane{o}", align_bytes=256) for o in range(PASSES)]
         for o in range(PASSES):
             nc.vector.memset(planes[o][:].bitcast(I32), 0)
-        picked = pool.tile([P, SLOTS], U8, name="picked", align_bytes=64)
+        picked = pool.tile([P, SLOTS], U8, name="picked", align_bytes=256)
         nc.vector.tensor_copy(picked[:], pool_scales[:].indirect(offsets[:]))
         nc.vector.tensor_copy(planes[0][:].bitcast(I32)[0:32], picked[:].bitcast(I32)[0:32])
         for o in range(PASSES):
@@ -57,7 +57,7 @@ def tile_attend_sddmm_kernel(tc, qT, k_words, k_scales, offs, out):
                         planes[o][:].bitcast(I32)[32 * quad:32 * quad + 4], picked[:].bitcast(I32)[first:first + 4]
                     )
 
-        row = pool.tile([P, POOL], F32, name="row")
+        row = pool.tile([P, POOL], F32, name="row", align_bytes=256)
         nc.vector.memset(row[:], 0.0)
 
         q_codes = [pool.tile([P, QUERIES], U32, name=f"q_codes{o}", align_bytes=64) for o in range(PASSES)]
@@ -74,7 +74,7 @@ def tile_attend_sddmm_kernel(tc, qT, k_words, k_scales, offs, out):
             nc.vector.quantize_mx(out=q_codes[o][:].bitcast(FP8X4), scales=q_scales[o][:], in_=q_bf[o][:])
 
         def part(name, tag, first, count):
-            words = pool.tile([P, PASSES * count], U16, name=name, tag=tag, align_bytes=64)
+            words = pool.tile([P, PASSES * count], U16, name=name, tag=tag, align_bytes=256)
             nc.vector.tensor_copy(
                 words[:].rearrange("p (o n) -> p o n", o=PASSES),
                 pairs[:, first:first + count].bitcast(U16).rearrange("p (n o) -> p o n", o=PASSES),
@@ -114,7 +114,7 @@ def tile_attend_sddmm_kernel(tc, qT, k_words, k_scales, offs, out):
         first_words = part("first_words", "q_raw0", 0, GROUP)
         quantise(1)
         first_scores = score("first_scores", first_words, 0, (0, 1))
-        other_tile = pool.tile([P, PASSES * (SLOTS - GROUP)], U16, name="other_words", tag="q_raw1", align_bytes=64)
+        other_tile = pool.tile([P, PASSES * (SLOTS - GROUP)], U16, name="other_words", tag="q_raw1", align_bytes=256)
         other_words = [other_tile[:, o * (SLOTS - GROUP):(o + 1) * (SLOTS - GROUP)] for o in range(PASSES)]
         for o in (1, 0):
             nc.vector.tensor_copy(other_words[o], pairs[:, GROUP:SLOTS].bitcast(U16)[:, o::PASSES])

@@ -19,7 +19,9 @@ POOL = 2048
 QUERIES = 128
 HALF = 256
 GROUP = 128
-SCALAR_SHARE = 16
+SCALAR_SHARE = 24
+EARLY = 256
+PIECES = (256,) * 8
 FLOPS = 2 * QUERIES * SLOTS * PASSES * P * PACK
 
 
@@ -32,8 +34,11 @@ def tile_attend_sddmm_kernel(tc, qT, k_words, k_scales, offs, out):
         offsets = pool.tile([P, SLOTS // 16], U16, name="offsets")
 
         q_rows = qT[0].rearrange("(o p j) n -> o p (j n)", o=PASSES, j=PACK)
-        q_raw = [pool.tile([P, PACK * QUERIES], F32, name=f"q_raw{o}", tag=f"q_raw{o}", align_bytes=256) for o in range(PASSES)]
-        pool_scales = pool.tile([P, POOL], U8, name="pool_scales", align_bytes=256)
+        q_raw = [
+            pool.tile([P, PACK * QUERIES], F32, name=f"q_raw{o}", tag=f"q_raw{o}", align_bytes=256)
+            for o in range(PASSES)
+        ]
+        pool_scales = pool.tile([P, POOL], U8, name="pool_scales", tag="window", align_bytes=256)
         pool_words = pool.tile([P, POOL], U32, name="pool_words", align_bytes=256)
         nc.vector.memset(pool_scales[:].bitcast(I32)[32:64], 0)
         nc.vector.memset(pool_scales[:].bitcast(I32)[64:P], 0)
@@ -46,8 +51,13 @@ def tile_attend_sddmm_kernel(tc, qT, k_words, k_scales, offs, out):
         planes = [pool.tile([P, SLOTS], U8, name=f"plane{o}", align_bytes=256) for o in range(PASSES)]
         for o in range(PASSES):
             nc.vector.memset(planes[o][:].bitcast(I32), 0)
+        scalar_row = pool.tile([P, POOL], F32, name="scalar_row", align_bytes=256)
+        nc.vector.memset(scalar_row[:], 0.0)
+        vector_row = pool.tile([P, POOL], F32, name="vector_row", align_bytes=256)
+        nc.vector.memset(vector_row[:, 0:EARLY], 0.0)
         picked = pool.tile([P, SLOTS], U8, name="picked", align_bytes=256)
         nc.vector.tensor_copy(picked[:], pool_scales[:].indirect(offsets[:]))
+        nc.vector.memset(vector_row[:, EARLY:POOL], 0.0)
         nc.vector.tensor_copy(planes[0][:].bitcast(I32)[0:32], picked[:].bitcast(I32)[0:32])
         for o in range(PASSES):
             for quad in range(4):
@@ -57,49 +67,12 @@ def tile_attend_sddmm_kernel(tc, qT, k_words, k_scales, offs, out):
                         planes[o][:].bitcast(I32)[32 * quad:32 * quad + 4], picked[:].bitcast(I32)[first:first + 4]
                     )
 
-        row = pool.tile([P, POOL], F32, name="row", align_bytes=256)
-        nc.vector.memset(row[:], 0.0)
-
         q_codes = [pool.tile([P, QUERIES], U32, name=f"q_codes{o}", align_bytes=64) for o in range(PASSES)]
         q_scales = [pool.tile([P, QUERIES], U8, name=f"q_scales{o}", align_bytes=64) for o in range(PASSES)]
-        q_bf = [pool.tile([P, QUERIES * PACK], BF16, name=f"q_bf{o}", tag=f"q_bf{o}", align_bytes=64) for o in range(PASSES)]
-
-        def cast(copy, o, first, last):
-            copy(
-                q_bf[o][:].rearrange("p (c i j) -> p c j i", i=4, j=PACK)[:, first:last],
-                q_raw[o][:].rearrange("p (j c i) -> p c j i", j=PACK, i=4)[:, first:last],
-            )
+        q_bf = [pool.tile([P, QUERIES * PACK], BF16, name=f"q_bf{o}", align_bytes=64) for o in range(PASSES)]
 
         def quantise(o):
             nc.vector.quantize_mx(out=q_codes[o][:].bitcast(FP8X4), scales=q_scales[o][:], in_=q_bf[o][:])
-
-        def part(name, tag, first, count):
-            words = pool.tile([P, PASSES * count], U16, name=name, tag=tag, align_bytes=256)
-            nc.vector.tensor_copy(
-                words[:].rearrange("p (o n) -> p o n", o=PASSES),
-                pairs[:, first:first + count].bitcast(U16).rearrange("p (n o) -> p o n", o=PASSES),
-            )
-            return [words[:, o * count:(o + 1) * count] for o in range(PASSES)]
-
-        def score(name, words, first, order):
-            count = words[0].shape[1]
-            staged = pool.tile([P, count], F32, name=name)
-            accs = [psum.tile([P, GROUP], F32, name=f"acc{first + c}") for c in range(0, count, GROUP)]
-            for step, o in enumerate(order):
-                for g, acc in enumerate(accs):
-                    cols = slice(g * GROUP, (g + 1) * GROUP)
-                    nc.tensor.matmul_mx(
-                        out=acc[:],
-                        lhsT=q_codes[o][:].bitcast(FP8X4),
-                        lhsT_scale=q_scales[o][:],
-                        rhs=words[o][:, cols].bitcast(FP4X4),
-                        rhs_scale=planes[o][:, first + g * GROUP:first + (g + 1) * GROUP],
-                        start=(step == 0),
-                        stop=(step == PASSES - 1),
-                    )
-                    if step == PASSES - 1:
-                        nc.scalar.copy(staged[:, cols], acc[:])
-            return staged
 
         pairs = pool.tile([P, SLOTS], U32, name="pairs", align_bytes=64)
         for h in range(SLOTS // HALF):
@@ -107,22 +80,76 @@ def tile_attend_sddmm_kernel(tc, qT, k_words, k_scales, offs, out):
                 pairs[:, h * HALF:(h + 1) * HALF],
                 pool_words[:].indirect(offsets[:, h * HALF // 16:(h + 1) * HALF // 16]),
             )
+        words = dict()
+
+        def cast(copy, o, first, last):
+            copy(
+                q_bf[o][:].rearrange("p (c i j) -> p c j i", i=4, j=PACK)[:, first:last],
+                q_raw[o][:].rearrange("p (j c i) -> p c j i", j=PACK, i=4)[:, first:last],
+            )
+
+        def part(name, tag, o, first, last):
+            place = pool.tile([P, last - first], U16, name=name, tag=tag, align_bytes=256)
+            nc.vector.tensor_copy(place[:], pairs[:, first:last].bitcast(U16)[:, o::PASSES])
+            for start in range(first, last, GROUP):
+                words.setdefault((o, start), place[:, start - first:start - first + GROUP])
+
         cast(nc.scalar.copy, 0, 0, QUERIES // 4)
         cast(nc.scalar.copy, 1, 0, SCALAR_SHARE)
-        cast(nc.vector.tensor_copy, 1, SCALAR_SHARE, QUERIES // 4)
+        part("words_a", "words_a", 0, 0, HALF)
         quantise(0)
-        first_words = part("first_words", "q_raw0", 0, GROUP)
+        cast(nc.vector.tensor_copy, 1, SCALAR_SHARE, QUERIES // 4)
+        part("words_b", "q_raw0", 0, HALF, HALF + GROUP)
         quantise(1)
-        first_scores = score("first_scores", first_words, 0, (0, 1))
-        other_tile = pool.tile([P, PASSES * (SLOTS - GROUP)], U16, name="other_words", tag="q_raw1", align_bytes=256)
-        other_words = [other_tile[:, o * (SLOTS - GROUP):(o + 1) * (SLOTS - GROUP)] for o in range(PASSES)]
-        for o in (1, 0):
-            nc.vector.tensor_copy(other_words[o], pairs[:, GROUP:SLOTS].bitcast(U16)[:, o::PASSES])
-        other_scores = score("other_scores", other_words, GROUP, (1, 0))
+        late = pool.tile([P, SLOTS + GROUP], U16, name="late", tag="q_raw1", align_bytes=256)
+        for o, first, last, place in ((1, 0, HALF, 0), (1, HALF, SLOTS, HALF), (0, SLOTS - GROUP, SLOTS, SLOTS)):
+            nc.vector.tensor_copy(late[:, place:place + last - first], pairs[:, first:last].bitcast(U16)[:, o::PASSES])
+            for start in range(first, last, GROUP):
+                words.setdefault((o, start), late[:, place + start - first:place + start - first + GROUP])
+
+        groups = [slice(first, first + GROUP) for first in range(0, SLOTS, GROUP)]
+        accs = [psum.tile([P, GROUP], F32, name=f"acc{cols.start}") for cols in groups]
+
+        def multiply(o, g, start):
+            nc.tensor.matmul_mx(
+                out=accs[g][:],
+                lhsT=q_codes[o][:].bitcast(FP8X4),
+                lhsT_scale=q_scales[o][:],
+                rhs=words[o, groups[g].start].bitcast(FP4X4),
+                rhs_scale=planes[o][:, groups[g]],
+                start=start,
+                stop=not start,
+            )
+
+        last = len(groups) - 1
+        for o in range(PASSES):
+            for g in range(last):
+                multiply(o, g, o == 0)
+        multiply(1, last, True)
+        multiply(0, last, False)
+
+        scores = pool.tile([P, SLOTS], F32, name="scores")
+        for acc, cols in zip(accs, groups):
+            nc.scalar.copy(scores[:, cols], acc[:])
         zeros = pool.tile([P, GROUP], F32, name="zeros")
         nc.vector.memset(zeros[:], 0.0)
-        nc.vector.tensor_tensor(
-            row[:].indirect(offsets[:, 0:GROUP // 16]), first_scores[:], zeros[:], mybir.AluOpType.add
+        for cols in (groups[0], groups[-1]):
+            nc.vector.tensor_tensor(
+                vector_row[:].indirect(offsets[:, cols.start // 16:cols.stop // 16]),
+                scores[:, cols],
+                zeros[:],
+                mybir.AluOpType.add,
+            )
+        nc.scalar.activation(
+            scalar_row[:].indirect(offsets[:, GROUP // 16:(SLOTS - GROUP) // 16]),
+            scores[:, GROUP:SLOTS - GROUP],
+            mybir.ActivationFunctionType.Copy,
         )
-        nc.vector.tensor_copy(row[:].indirect(offsets[:, GROUP // 16:SLOTS // 16]), other_scores[:])
-        nc.sync.dma_start(out[0], row[:])
+
+        first = 0
+        for width in PIECES:
+            cols = slice(first, first + width)
+            piece = pool.tile([P, width], F32, name=f"piece{first}", align_bytes=256)
+            nc.vector.tensor_tensor(piece[:], scalar_row[:, cols], vector_row[:, cols], mybir.AluOpType.add)
+            nc.sync.dma_start(out[0][:, cols], piece[:])
+            first += width

@@ -21,7 +21,7 @@ HALF = 256
 GROUP = 128
 SCALAR_SHARE = 24
 EARLY = 256
-PIECES = (256,) * 8
+PIECES = (256,) * 7 + (128, 128)
 FLOPS = 2 * QUERIES * SLOTS * PASSES * P * PACK
 
 
@@ -132,7 +132,7 @@ def tile_attend_sddmm_kernel(tc, qT, k_words, k_scales, offs, out):
         for acc, cols in zip(accs, groups):
             nc.scalar.copy(scores[:, cols], acc[:])
         zeros = pool.tile([P, GROUP], F32, name="zeros")
-        nc.vector.memset(zeros[:], 0.0)
+        nc.scalar.copy(zeros[:], scalar_row[:, 0:GROUP])
         for cols in (groups[0], groups[-1]):
             nc.vector.tensor_tensor(
                 vector_row[:].indirect(offsets[:, cols.start // 16:cols.stop // 16]),

@@ -19,7 +19,7 @@ POOL = 2048
 QUERIES = 128
 HALF = 256
 GROUP = 128
-SCALAR_SHARE = 24
+SCALAR_SHARE = 20
 EARLY = 256
 PIECES = (256,) * 7 + (128, 128)
 FLOPS = 2 * QUERIES * SLOTS * PASSES * P * PACK
@@ -99,13 +99,19 @@ def tile_attend_sddmm_kernel(tc, qT, k_words, k_scales, offs, out):
         part("words_a", "words_a", 0, 0, HALF)
         quantise(0)
         cast(nc.vector.tensor_copy, 1, SCALAR_SHARE, QUERIES // 4)
-        part("words_b", "q_raw0", 0, HALF, HALF + GROUP)
+        middle = pool.tile([P, PASSES * GROUP], U16, name="middle", tag="q_raw0", align_bytes=256)
+        for o, first, place in ((0, HALF, 0), (1, 0, GROUP)):
+            nc.vector.tensor_copy(middle[:, place:place + GROUP], pairs[:, first:first + GROUP].bitcast(U16)[:, o::PASSES])
+            words.setdefault((o, first), middle[:, place:place + GROUP])
         quantise(1)
-        late = pool.tile([P, SLOTS + GROUP], U16, name="late", tag="q_raw1", align_bytes=256)
-        for o, first, last, place in ((1, 0, HALF, 0), (1, HALF, SLOTS, HALF), (0, SLOTS - GROUP, SLOTS, SLOTS)):
-            nc.vector.tensor_copy(late[:, place:place + last - first], pairs[:, first:last].bitcast(U16)[:, o::PASSES])
-            for start in range(first, last, GROUP):
-                words.setdefault((o, start), late[:, place + start - first:place + start - first + GROUP])
+        late = pool.tile([P, SLOTS], U16, name="late", tag="q_raw1", align_bytes=256)
+        nc.vector.tensor_copy(late[:, 0:HALF], pairs[:, GROUP:GROUP + HALF].bitcast(U16)[:, 1::PASSES])
+        nc.vector.tensor_copy(
+            late[:, HALF:SLOTS].rearrange("p (o n) -> p o n", o=PASSES),
+            pairs[:, SLOTS - GROUP:SLOTS].bitcast(U16).rearrange("p (n o) -> p o n", o=PASSES),
+        )
+        for key, place in (((1, GROUP), 0), ((1, HALF), GROUP), ((0, SLOTS - GROUP), HALF), ((1, SLOTS - GROUP), HALF + GROUP)):
+            words.setdefault(key, late[:, place:place + GROUP])
 
         groups = [slice(first, first + GROUP) for first in range(0, SLOTS, GROUP)]
         accs = [psum.tile([P, GROUP], F32, name=f"acc{cols.start}") for cols in groups]

@@ -21,6 +21,7 @@ HALF = 256
 GROUP = 128
 SCALAR_SHARE = 20
 EARLY = 256
+LEAD = 64
 PIECES = (256,) * 7 + (128, 128)
 FLOPS = 2 * QUERIES * SLOTS * PASSES * P * PACK
 
@@ -134,21 +135,23 @@ def tile_attend_sddmm_kernel(tc, qT, k_words, k_scales, offs, out):
         multiply(1, last, True)
         multiply(0, last, False)
 
+        zeros = pool.tile([P, HALF - LEAD], F32, name="zeros")
+        nc.scalar.copy(zeros[:], scalar_row[:, 0:HALF - LEAD])
         scores = pool.tile([P, SLOTS], F32, name="scores")
-        for acc, cols in zip(accs, groups):
+        nc.scalar.copy(scores[:, 0:LEAD], accs[0][:, 0:LEAD])
+        nc.scalar.copy(scores[:, LEAD:GROUP], accs[0][:, LEAD:GROUP])
+        for acc, cols in zip(accs[1:], groups[1:]):
             nc.scalar.copy(scores[:, cols], acc[:])
-        zeros = pool.tile([P, GROUP], F32, name="zeros")
-        nc.scalar.copy(zeros[:], scalar_row[:, 0:GROUP])
-        for cols in (groups[0], groups[-1]):
+        for cols in (slice(0, LEAD), slice(LEAD + HALF, SLOTS)):
             nc.vector.tensor_tensor(
                 vector_row[:].indirect(offsets[:, cols.start // 16:cols.stop // 16]),
                 scores[:, cols],
-                zeros[:],
+                zeros[:, 0:cols.stop - cols.start],
                 mybir.AluOpType.add,
             )
         nc.scalar.activation(
-            scalar_row[:].indirect(offsets[:, GROUP // 16:(SLOTS - GROUP) // 16]),
-            scores[:, GROUP:SLOTS - GROUP],
+            scalar_row[:].indirect(offsets[:, LEAD // 16:(LEAD + HALF) // 16]),
+            scores[:, LEAD:LEAD + HALF],
             mybir.ActivationFunctionType.Copy,
         )
 

@@ -22,7 +22,7 @@ GROUP = 128
 SCALAR_SHARE = 20
 EARLY = 256
 LEAD = 64
-PIECES = (256,) * 7 + (128, 128)
+PIECES = (128,) + (256,) * 7 + (128,)
 FLOPS = 2 * QUERIES * SLOTS * PASSES * P * PACK
 
 

@@ -30,6 +30,7 @@ def tile_attend_sddmm_kernel(tc, qT, k_words, k_scales, offs, out):
     nc = tc.nc
     with ExitStack() as ctx:
         pool = ctx.enter_context(tc.tile_pool(name="pool", bufs=1))
+        shared = ctx.enter_context(tc.tile_pool(name="shared", bufs=1))
         psum = ctx.enter_context(tc.psum_pool(name="psum", bufs=1))
 
         offsets = pool.tile([P, SLOTS // 16], U16, name="offsets")
@@ -39,7 +40,7 @@ def tile_attend_sddmm_kernel(tc, qT, k_words, k_scales, offs, out):
             pool.tile([P, PACK * QUERIES], F32, name=f"q_raw{o}", tag=f"q_raw{o}", align_bytes=256)
             for o in range(PASSES)
         ]
-        pool_scales = pool.tile([P, POOL], U8, name="pool_scales", tag="window", align_bytes=256)
+        pool_scales = shared.tile([P, POOL], U8, name="pool_scales", offset=0, align_bytes=256)
         pool_words = pool.tile([P, POOL], U32, name="pool_words", align_bytes=256)
         nc.vector.memset(pool_scales[:].bitcast(I32)[32:64], 0)
         nc.vector.memset(pool_scales[:].bitcast(I32)[64:P], 0)
@@ -49,9 +50,6 @@ def tile_attend_sddmm_kernel(tc, qT, k_words, k_scales, offs, out):
         for o in range(PASSES):
             nc.sync.dma_start(q_raw[o][:], q_rows[o])
 
-        planes = [pool.tile([P, SLOTS], U8, name=f"plane{o}", align_bytes=256) for o in range(PASSES)]
-        for o in range(PASSES):
-            nc.vector.memset(planes[o][:].bitcast(I32), 0)
         scalar_row = pool.tile([P, POOL], F32, name="scalar_row", align_bytes=256)
         nc.vector.memset(scalar_row[:], 0.0)
         vector_row = pool.tile([P, POOL], F32, name="vector_row", align_bytes=256)
@@ -59,6 +57,9 @@ def tile_attend_sddmm_kernel(tc, qT, k_words, k_scales, offs, out):
         picked = pool.tile([P, SLOTS], U8, name="picked", align_bytes=256)
         nc.vector.tensor_copy(picked[:], pool_scales[:].indirect(offsets[:]))
         nc.vector.memset(vector_row[:, EARLY:POOL], 0.0)
+        planes = [
+            shared.tile([P, SLOTS], U8, name=f"plane{o}", offset=o * SLOTS, align_bytes=256) for o in range(PASSES)
+        ]
         nc.vector.tensor_copy(planes[0][:].bitcast(I32)[0:32], picked[:].bitcast(I32)[0:32])
         for o in range(PASSES):
             for quad in range(4):

@@ -46,7 +46,7 @@ def tile_attend_sddmm_kernel(tc, qT, k_words, k_scales, offs, out):
         nc.vector.memset(pool_scales[:].bitcast(I32)[64:P], 0)
         nc.sync.dma_start(pool_scales[:].bitcast(I32)[0:32], k_scales.bitcast(I32).rearrange("o f t -> (o f) t"))
         nc.sync.dma_start(offsets[:], offs)
-        nc.sync.dma_start(pool_words[:].bitcast(I32), k_words[0].rearrange("p t b -> p (t b)").bitcast(I32))
+        nc.sync.dma_start(pool_words[:].bitcast(I32), k_words[0].rearrange("p t b -> p (t b)").bitcast(I32), max_dma_last_dim=4096)
         for o in range(PASSES):
             nc.sync.dma_start(q_raw[o][:], q_rows[o])
 

@@ -69,14 +69,14 @@ def tile_attend_sddmm_kernel(tc, qT, k_words, k_scales, offs, out):
                         planes[o][:].bitcast(I32)[32 * quad:32 * quad + 4], picked[:].bitcast(I32)[first:first + 4]
                     )
 
-        q_codes = [pool.tile([P, QUERIES], U32, name=f"q_codes{o}", align_bytes=64) for o in range(PASSES)]
-        q_scales = [pool.tile([P, QUERIES], U8, name=f"q_scales{o}", align_bytes=64) for o in range(PASSES)]
-        q_bf = [pool.tile([P, QUERIES * PACK], BF16, name=f"q_bf{o}", align_bytes=64) for o in range(PASSES)]
+        q_codes = [pool.tile([P, QUERIES], U32, name=f"q_codes{o}", align_bytes=256) for o in range(PASSES)]
+        q_scales = [pool.tile([P, QUERIES], U8, name=f"q_scales{o}", align_bytes=256) for o in range(PASSES)]
+        q_bf = [pool.tile([P, QUERIES * PACK], BF16, name=f"q_bf{o}", align_bytes=256) for o in range(PASSES)]
 
         def quantise(o):
             nc.vector.quantize_mx(out=q_codes[o][:].bitcast(FP8X4), scales=q_scales[o][:], in_=q_bf[o][:])
 
-        pairs = pool.tile([P, SLOTS], U32, name="pairs", align_bytes=64)
+        pairs = pool.tile([P, SLOTS], U32, name="pairs", align_bytes=256)
         for h in range(SLOTS // HALF):
             nc.vector.tensor_copy(
                 pairs[:, h * HALF:(h + 1) * HALF],
@@ -136,9 +136,9 @@ def tile_attend_sddmm_kernel(tc, qT, k_words, k_scales, offs, out):
         multiply(1, last, True)
         multiply(0, last, False)
 
-        zeros = pool.tile([P, HALF - LEAD], F32, name="zeros")
+        zeros = pool.tile([P, HALF - LEAD], F32, name="zeros", align_bytes=256)
         nc.scalar.copy(zeros[:], scalar_row[:, 0:HALF - LEAD])
-        scores = pool.tile([P, SLOTS], F32, name="scores")
+        scores = pool.tile([P, SLOTS], F32, name="scores", align_bytes=256)
         nc.scalar.copy(scores[:, 0:LEAD], accs[0][:, 0:LEAD])
         nc.scalar.copy(scores[:, LEAD:GROUP], accs[0][:, LEAD:GROUP])
         for acc, cols in zip(accs[1:], groups[1:]):

@@ -19,7 +19,7 @@ POOL = 2048
 QUERIES = 128
 HALF = 256
 GROUP = 128
-SCALAR_SHARE = 20
+SCALAR_SHARE = 24
 EARLY = 256
 LEAD = 64
 PIECES = (128,) + (256,) * 7 + (128,)

@@ -22,6 +22,7 @@ GROUP = 128
 SCALAR_SHARE = 24
 EARLY = 256
 LEAD = 64
+ROWS_AT = 96
 PIECES = (128,) + (256,) * 7 + (128,)
 FLOPS = 2 * QUERIES * SLOTS * PASSES * P * PACK
 
@@ -42,9 +43,8 @@ def tile_attend_sddmm_kernel(tc, qT, k_words, k_scales, offs, out):
         ]
         pool_scales = shared.tile([P, POOL], U8, name="pool_scales", offset=0, align_bytes=256)
         pool_words = pool.tile([P, POOL], U32, name="pool_words", align_bytes=256)
-        nc.vector.memset(pool_scales[:].bitcast(I32)[32:64], 0)
-        nc.vector.memset(pool_scales[:].bitcast(I32)[64:P], 0)
-        nc.sync.dma_start(pool_scales[:].bitcast(I32)[0:32], k_scales.bitcast(I32).rearrange("o f t -> (o f) t"))
+        nc.vector.memset(pool_scales[:].bitcast(I32)[0:ROWS_AT], 0)
+        nc.sync.dma_start(pool_scales[:].bitcast(I32)[ROWS_AT:P], k_scales.bitcast(I32).rearrange("o f t -> (o f) t"))
         nc.sync.dma_start(offsets[:], offs)
         nc.sync.dma_start(pool_words[:].bitcast(I32), k_words[0].rearrange("p t b -> p (t b)").bitcast(I32), max_dma_last_dim=4096)
         for o in range(PASSES):
@@ -60,13 +60,13 @@ def tile_attend_sddmm_kernel(tc, qT, k_words, k_scales, offs, out):
         planes = [
             shared.tile([P, SLOTS], U8, name=f"plane{o}", offset=o * SLOTS, align_bytes=256) for o in range(PASSES)
         ]
-        nc.vector.tensor_copy(planes[0][:].bitcast(I32)[0:32], picked[:].bitcast(I32)[0:32])
+        nc.vector.tensor_copy(planes[0][:].bitcast(I32)[0:32], picked[:].bitcast(I32)[ROWS_AT:P])
         for o in range(PASSES):
             for quad in range(4):
                 first = 16 * o + 4 * quad
                 if first > 0:
                     nc.sync.dma_start(
-                        planes[o][:].bitcast(I32)[32 * quad:32 * quad + 4], picked[:].bitcast(I32)[first:first + 4]
+                        planes[o][:].bitcast(I32)[32 * quad:32 * quad + 4], picked[:].bitcast(I32)[ROWS_AT + first:ROWS_AT + first + 4]
                     )
 
         q_codes = [pool.tile([P, QUERIES], U32, name=f"q_codes{o}", align_bytes=256) for o in range(PASSES)]

from contextlib import ExitStack

import concourse.mybir as mybir

F32 = mybir.dt.float32
BF16 = mybir.dt.bfloat16
I32 = mybir.dt.int32
U32 = mybir.dt.uint32
U16 = mybir.dt.uint16
U8 = mybir.dt.uint8
FP8X4 = mybir.dt.float8_e4m3fn_x4
FP4X4 = mybir.dt.float4_e2m1fn_x4

P = 128
PACK = 4
PASSES = 2
SLOTS = 512
POOL = 2048
QUERIES = 128
HALF = 256
GROUP = 128
SCALAR_SHARE = 24
EARLY = 256
LEAD = 64
ROWS_AT = 96
PIECES = (128,) + (256,) * 7 + (128,)
FLOPS = 2 * QUERIES * SLOTS * PASSES * P * PACK


def tile_attend_sddmm_kernel(tc, qT, k_words, k_scales, offs, out):
    nc = tc.nc
    with ExitStack() as ctx:
        pool = ctx.enter_context(tc.tile_pool(name="pool", bufs=1))
        shared = ctx.enter_context(tc.tile_pool(name="shared", bufs=1))
        psum = ctx.enter_context(tc.psum_pool(name="psum", bufs=1))

        offsets = pool.tile([P, SLOTS // 16], U16, name="offsets")

        q_rows = qT[0].rearrange("(o p j) n -> o p (j n)", o=PASSES, j=PACK)
        q_raw = [
            pool.tile([P, PACK * QUERIES], F32, name=f"q_raw{o}", tag=f"q_raw{o}", align_bytes=256)
            for o in range(PASSES)
        ]
        pool_scales = shared.tile([P, POOL], U8, name="pool_scales", offset=0, align_bytes=256)
        pool_words = pool.tile([P, POOL], U32, name="pool_words", align_bytes=256)
        nc.vector.memset(pool_scales[:].bitcast(I32)[0:ROWS_AT], 0)
        nc.sync.dma_start(pool_scales[:].bitcast(I32)[ROWS_AT:P], k_scales.bitcast(I32).rearrange("o f t -> (o f) t"))
        nc.sync.dma_start(offsets[:], offs)
        nc.sync.dma_start(pool_words[:].bitcast(I32), k_words[0].rearrange("p t b -> p (t b)").bitcast(I32), max_dma_last_dim=4096)
        for o in range(PASSES):
            nc.sync.dma_start(q_raw[o][:], q_rows[o])

        scalar_row = pool.tile([P, POOL], F32, name="scalar_row", align_bytes=256)
        nc.vector.memset(scalar_row[:], 0.0)
        vector_row = pool.tile([P, POOL], F32, name="vector_row", align_bytes=256)
        nc.vector.memset(vector_row[:, 0:EARLY], 0.0)
        picked = pool.tile([P, SLOTS], U8, name="picked", align_bytes=256)
        nc.vector.tensor_copy(picked[:], pool_scales[:].indirect(offsets[:]))
        nc.vector.memset(vector_row[:, EARLY:POOL], 0.0)
        planes = [
            shared.tile([P, SLOTS], U8, name=f"plane{o}", offset=o * SLOTS, align_bytes=256) for o in range(PASSES)
        ]
        nc.vector.tensor_copy(planes[0][:].bitcast(I32)[0:32], picked[:].bitcast(I32)[ROWS_AT:P])
        for o in range(PASSES):
            for quad in range(4):
                first = 16 * o + 4 * quad
                if first > 0:
                    nc.sync.dma_start(
                        planes[o][:].bitcast(I32)[32 * quad:32 * quad + 4], picked[:].bitcast(I32)[ROWS_AT + first:ROWS_AT + first + 4]
                    )

        q_codes = [pool.tile([P, QUERIES], U32, name=f"q_codes{o}", align_bytes=256) for o in range(PASSES)]
        q_scales = [pool.tile([P, QUERIES], U8, name=f"q_scales{o}", align_bytes=256) for o in range(PASSES)]
        q_bf = [pool.tile([P, QUERIES * PACK], BF16, name=f"q_bf{o}", align_bytes=256) for o in range(PASSES)]

        def quantise(o):
            nc.vector.quantize_mx(out=q_codes[o][:].bitcast(FP8X4), scales=q_scales[o][:], in_=q_bf[o][:])

        pairs = pool.tile([P, SLOTS], U32, name="pairs", align_bytes=256)
        for h in range(SLOTS // HALF):
            nc.vector.tensor_copy(
                pairs[:, h * HALF:(h + 1) * HALF],
                pool_words[:].indirect(offsets[:, h * HALF // 16:(h + 1) * HALF // 16]),
            )
        words = dict()

        def cast(copy, o, first, last):
            copy(
                q_bf[o][:].rearrange("p (c i j) -> p c j i", i=4, j=PACK)[:, first:last],
                q_raw[o][:].rearrange("p (j c i) -> p c j i", j=PACK, i=4)[:, first:last],
            )

        def part(name, tag, o, first, last):
            place = pool.tile([P, last - first], U16, name=name, tag=tag, align_bytes=256)
            nc.vector.tensor_copy(place[:], pairs[:, first:last].bitcast(U16)[:, o::PASSES])
            for start in range(first, last, GROUP):
                words.setdefault((o, start), place[:, start - first:start - first + GROUP])

        cast(nc.scalar.copy, 0, 0, QUERIES // 4)
        cast(nc.scalar.copy, 1, 0, SCALAR_SHARE)
        part("words_a", "words_a", 0, 0, HALF)
        quantise(0)
        cast(nc.vector.tensor_copy, 1, SCALAR_SHARE, QUERIES // 4)
        middle = pool.tile([P, PASSES * GROUP], U16, name="middle", tag="q_raw0", align_bytes=256)
        for o, first, place in ((0, HALF, 0), (1, 0, GROUP)):
            nc.vector.tensor_copy(middle[:, place:place + GROUP], pairs[:, first:first + GROUP].bitcast(U16)[:, o::PASSES])
            words.setdefault((o, first), middle[:, place:place + GROUP])
        quantise(1)
        late = pool.tile([P, SLOTS], U16, name="late", tag="q_raw1", align_bytes=256)
        nc.vector.tensor_copy(late[:, 0:HALF], pairs[:, GROUP:GROUP + HALF].bitcast(U16)[:, 1::PASSES])
        nc.vector.tensor_copy(
            late[:, HALF:SLOTS].rearrange("p (o n) -> p o n", o=PASSES),
            pairs[:, SLOTS - GROUP:SLOTS].bitcast(U16).rearrange("p (n o) -> p o n", o=PASSES),
        )
        for key, place in (((1, GROUP), 0), ((1, HALF), GROUP), ((0, SLOTS - GROUP), HALF), ((1, SLOTS - GROUP), HALF + GROUP)):
            words.setdefault(key, late[:, place:place + GROUP])

        groups = [slice(first, first + GROUP) for first in range(0, SLOTS, GROUP)]
        accs = [psum.tile([P, GROUP], F32, name=f"acc{cols.start}") for cols in groups]

        def multiply(o, g, start):
            nc.tensor.matmul_mx(
                out=accs[g][:],
                lhsT=q_codes[o][:].bitcast(FP8X4),
                lhsT_scale=q_scales[o][:],
                rhs=words[o, groups[g].start].bitcast(FP4X4),
                rhs_scale=planes[o][:, groups[g]],
                start=start,
                stop=not start,
            )

        last = len(groups) - 1
        for o in range(PASSES):
            for g in range(last):
                multiply(o, g, o == 0)
        multiply(1, last, True)
        multiply(0, last, False)

        zeros = pool.tile([P, HALF - LEAD], F32, name="zeros", align_bytes=256)
        nc.scalar.copy(zeros[:], scalar_row[:, 0:HALF - LEAD])
        scores = pool.tile([P, SLOTS], F32, name="scores", align_bytes=256)
        nc.scalar.copy(scores[:, 0:LEAD], accs[0][:, 0:LEAD])
        nc.scalar.copy(scores[:, LEAD:GROUP], accs[0][:, LEAD:GROUP])
        for acc, cols in zip(accs[1:], groups[1:]):
            nc.scalar.copy(scores[:, cols], acc[:])
        for cols in (slice(0, LEAD), slice(LEAD + HALF, SLOTS)):
            nc.vector.tensor_tensor(
                vector_row[:].indirect(offsets[:, cols.start // 16:cols.stop // 16]),
                scores[:, cols],
                zeros[:, 0:cols.stop - cols.start],
                mybir.AluOpType.add,
            )
        nc.scalar.activation(
            scalar_row[:].indirect(offsets[:, LEAD // 16:(LEAD + HALF) // 16]),
            scores[:, LEAD:LEAD + HALF],
            mybir.ActivationFunctionType.Copy,
        )

        first = 0
        for width in PIECES:
            cols = slice(first, first + width)
            piece = pool.tile([P, width], F32, name=f"piece{first}", align_bytes=256)
            nc.vector.tensor_tensor(piece[:], scalar_row[:, cols], vector_row[:, cols], mybir.AluOpType.add)
            nc.sync.dma_start(out[0][:, cols], piece[:])
            first += width
